import numpy as np
import ml_dtypes

BF16 = ml_dtypes.bfloat16


def bf(x):
    return np.asarray(x, np.float32).astype(BF16)


def f32(x):
    return np.asarray(x, np.float32)


def f64(x):
    return np.asarray(x).astype(np.float64)


def striped(idx):
    return np.tile(idx.reshape(-1, 16).T, (8, 1))


S, K, M, N = 256, 128, 512, 128


def setup_inputs():
    return {"base": bf(np.random.standard_normal((M, S))), "x": bf(np.random.standard_normal((K, N))), "w": bf(np.random.standard_normal((K, M)) / np.sqrt(K)), "offs": striped(np.random.permutation(S)[:N])}


def reference(base, x, w, offs):
    idx = offs[:16].T.reshape(-1)
    z = f64(base).copy()
    z[:, idx] = f64(w).T @ f64(x)
    return z

@@ -1,0 +1,55 @@
+import concourse.mybir as mybir
+from concourse.masks import make_identity
+
+P = 128
+BF16, F32, U16 = mybir.dt.bfloat16, mybir.dt.float32, mybir.dt.uint16
+
+FLOPS = 2 * 128 * 512 * 128
+
+
+def tile_scatter_matmul_kernel(tc, base, x, w, offs, out):
+    nc = tc.nc
+    features, tokens = base.shape
+    entries = x.shape[1]
+    blocks = features // P
+
+    with (
+        tc.tile_pool(name="held", bufs=1) as held,
+        tc.psum_pool(name="banks", bufs=1) as banks,
+    ):
+        offsets = held.tile([P, entries // 16], U16, name="offsets")
+        nc.sync.dma_start(offsets[:], offs)
+
+        ident = held.tile([P, P], BF16, name="ident")
+        make_identity(nc, ident[:])
+
+        base_tiles = [held.tile([P, tokens], BF16, name=f"base{a}") for a in range(blocks)]
+        for a in range(blocks):
+            queue = nc.sync if a % 2 == 0 else nc.scalar
+            queue.dma_start(base_tiles[a][:], base[a * P : (a + 1) * P, :])
+        x_tile = held.tile([P, entries], BF16, name="x_tile")
+        nc.sync.dma_start(x_tile[:], x)
+        w_tile = held.tile([P, features], BF16, name="w_tile")
+        nc.scalar.dma_start(w_tile[:], w)
+
+        windows = [banks.tile([P, tokens], F32, name=f"window{a}") for a in range(blocks)]
+        for a in range(blocks):
+            nc.tensor.matmul(windows[a][:], ident[:], base_tiles[a][:], start=True, stop=True)
+
+        for a in range(blocks):
+            nc.tensor.matmul(
+                windows[a][:].indirect(offsets[:]),
+                w_tile[:, a * P : (a + 1) * P],
+                x_tile[:],
+                start=True,
+                stop=True,
+            )
+
+        for a in range(blocks):
+            z_tile = held.tile([P, tokens], F32, name=f"z{a}")
+            if a % 2 == 0:
+                nc.vector.tensor_copy(z_tile[:], windows[a][:])
+                nc.sync.dma_start(out[a * P : (a + 1) * P, :], z_tile[:])
+            else:
+                nc.scalar.copy(z_tile[:], windows[a][:])
+                nc.scalar.dma_start(out[a * P : (a + 1) * P, :], z_tile[:])

@@ -6,6 +6,9 @@ BF16, F32, U16 = mybir.dt.bfloat16, mybir.dt.float32, mybir.dt.uint16
 
 FLOPS = 2 * 128 * 512 * 128
 
+WARM_COLUMNS = 512
+WARM_MATMULS = 4
+
 
 def tile_scatter_matmul_kernel(tc, base, x, w, offs, out):
     nc = tc.nc
@@ -31,6 +34,12 @@ def tile_scatter_matmul_kernel(tc, base, x, w, offs, out):
         nc.sync.dma_start(x_tile[:], x)
         w_tile = held.tile([P, features], BF16, name="w_tile")
         nc.scalar.dma_start(w_tile[:], w)
+
+        zeros = held.tile([P, WARM_COLUMNS], BF16, name="zeros")
+        nc.vector.memset(zeros[:], 0.0)
+        spare = banks.tile([P, WARM_COLUMNS], F32, name="spare")
+        for _ in range(WARM_MATMULS):
+            nc.tensor.matmul(spare[:], zeros[:, 0:P], zeros[:], start=True, stop=True)
 
         windows = [banks.tile([P, tokens], F32, name=f"window{a}") for a in range(blocks)]
         for a in range(blocks):

@@ -6,8 +6,8 @@ BF16, F32, U16 = mybir.dt.bfloat16, mybir.dt.float32, mybir.dt.uint16
 
 FLOPS = 2 * 128 * 512 * 128
 
-WARM_COLUMNS = 512
-WARM_MATMULS = 4
+WARM_COLUMNS = 128
+WARM_MATMULS = 10
 
 
 def tile_scatter_matmul_kernel(tc, base, x, w, offs, out):
@@ -23,6 +23,12 @@ def tile_scatter_matmul_kernel(tc, base, x, w, offs, out):
         offsets = held.tile([P, entries // 16], U16, name="offsets")
         nc.sync.dma_start(offsets[:], offs)
 
+        zeros = held.tile([P, WARM_COLUMNS], BF16, name="zeros")
+        nc.vector.memset(zeros[:], 0.0)
+        spare = banks.tile([P, WARM_COLUMNS], F32, name="spare")
+        for repeat in range(WARM_MATMULS):
+            nc.tensor.matmul(spare[:], zeros[:, 0:P], zeros[:], start=True, stop=True)
+
         ident = held.tile([P, P], BF16, name="ident")
         make_identity(nc, ident[:])
 
@@ -34,12 +40,6 @@ def tile_scatter_matmul_kernel(tc, base, x, w, offs, out):
         nc.sync.dma_start(x_tile[:], x)
         w_tile = held.tile([P, features], BF16, name="w_tile")
         nc.scalar.dma_start(w_tile[:], w)
-
-        zeros = held.tile([P, WARM_COLUMNS], BF16, name="zeros")
-        nc.vector.memset(zeros[:], 0.0)
-        spare = banks.tile([P, WARM_COLUMNS], F32, name="spare")
-        for _ in range(WARM_MATMULS):
-            nc.tensor.matmul(spare[:], zeros[:, 0:P], zeros[:], start=True, stop=True)
 
         windows = [banks.tile([P, tokens], F32, name=f"window{a}") for a in range(blocks)]
         for a in range(blocks):

@@ -38,8 +38,10 @@ def tile_scatter_matmul_kernel(tc, base, x, w, offs, out):
             queue.dma_start(base_tiles[a][:], base[a * P : (a + 1) * P, :])
         x_tile = held.tile([P, entries], BF16, name="x_tile")
         nc.sync.dma_start(x_tile[:], x)
-        w_tile = held.tile([P, features], BF16, name="w_tile")
-        nc.scalar.dma_start(w_tile[:], w)
+        w_tiles = [held.tile([P, P], BF16, name=f"w{a}") for a in range(blocks)]
+        for a in range(blocks):
+            queue = nc.scalar if a % 2 == 0 else nc.sync
+            queue.dma_start(w_tiles[a][:], w[:, a * P : (a + 1) * P])
 
         windows = [banks.tile([P, tokens], F32, name=f"window{a}") for a in range(blocks)]
         for a in range(blocks):
@@ -48,7 +50,7 @@ def tile_scatter_matmul_kernel(tc, base, x, w, offs, out):
         for a in range(blocks):
             nc.tensor.matmul(
                 windows[a][:].indirect(offsets[:]),
-                w_tile[:, a * P : (a + 1) * P],
+                w_tiles[a][:],
                 x_tile[:],
                 start=True,
                 stop=True,

@@ -38,10 +38,11 @@ def tile_scatter_matmul_kernel(tc, base, x, w, offs, out):
             queue.dma_start(base_tiles[a][:], base[a * P : (a + 1) * P, :])
         x_tile = held.tile([P, entries], BF16, name="x_tile")
         nc.sync.dma_start(x_tile[:], x)
-        w_tiles = [held.tile([P, P], BF16, name=f"w{a}") for a in range(blocks)]
-        for a in range(blocks):
-            queue = nc.scalar if a % 2 == 0 else nc.sync
-            queue.dma_start(w_tiles[a][:], w[:, a * P : (a + 1) * P])
+        w_first = held.tile([P, P], BF16, name="w_first")
+        nc.scalar.dma_start(w_first[:], w[:, 0:P])
+        w_rest = held.tile([P, features - P], BF16, name="w_rest")
+        nc.scalar.dma_start(w_rest[:], w[:, P:features])
+        w_blocks = [w_first[:]] + [w_rest[:, (a - 1) * P : a * P] for a in range(1, blocks)]
 
         windows = [banks.tile([P, tokens], F32, name=f"window{a}") for a in range(blocks)]
         for a in range(blocks):
@@ -50,7 +51,7 @@ def tile_scatter_matmul_kernel(tc, base, x, w, offs, out):
         for a in range(blocks):
             nc.tensor.matmul(
                 windows[a][:].indirect(offsets[:]),
-                w_tiles[a][:],
+                w_blocks[a],
                 x_tile[:],
                 start=True,
                 stop=True,

@@ -34,14 +34,13 @@ def tile_scatter_matmul_kernel(tc, base, x, w, offs, out):
 
         base_tiles = [held.tile([P, tokens], BF16, name=f"base{a}") for a in range(blocks)]
         for a in range(blocks):
-            queue = nc.sync if a % 2 == 0 else nc.scalar
-            queue.dma_start(base_tiles[a][:], base[a * P : (a + 1) * P, :])
+            nc.sync.dma_start(base_tiles[a][:], base[a * P : (a + 1) * P, :])
         x_tile = held.tile([P, entries], BF16, name="x_tile")
         nc.sync.dma_start(x_tile[:], x)
         w_first = held.tile([P, P], BF16, name="w_first")
-        nc.scalar.dma_start(w_first[:], w[:, 0:P])
+        nc.sync.dma_start(w_first[:], w[:, 0:P])
         w_rest = held.tile([P, features - P], BF16, name="w_rest")
-        nc.scalar.dma_start(w_rest[:], w[:, P:features])
+        nc.sync.dma_start(w_rest[:], w[:, P:features])
         w_blocks = [w_first[:]] + [w_rest[:, (a - 1) * P : a * P] for a in range(1, blocks)]
 
         windows = [banks.tile([P, tokens], F32, name=f"window{a}") for a in range(blocks)]

@@ -6,6 +6,8 @@ BF16, F32, U16 = mybir.dt.bfloat16, mybir.dt.float32, mybir.dt.uint16
 
 FLOPS = 2 * 128 * 512 * 128
 
+DMA_ALIGN = 256
+
 WARM_COLUMNS = 128
 WARM_MATMULS = 10
 
@@ -32,14 +34,14 @@ def tile_scatter_matmul_kernel(tc, base, x, w, offs, out):
         ident = held.tile([P, P], BF16, name="ident")
         make_identity(nc, ident[:])
 
-        base_tiles = [held.tile([P, tokens], BF16, name=f"base{a}") for a in range(blocks)]
+        base_tiles = [held.tile([P, tokens], BF16, name=f"base{a}", align_bytes=DMA_ALIGN) for a in range(blocks)]
         for a in range(blocks):
             nc.sync.dma_start(base_tiles[a][:], base[a * P : (a + 1) * P, :])
-        x_tile = held.tile([P, entries], BF16, name="x_tile")
+        x_tile = held.tile([P, entries], BF16, name="x_tile", align_bytes=DMA_ALIGN)
         nc.sync.dma_start(x_tile[:], x)
-        w_first = held.tile([P, P], BF16, name="w_first")
+        w_first = held.tile([P, P], BF16, name="w_first", align_bytes=DMA_ALIGN)
         nc.sync.dma_start(w_first[:], w[:, 0:P])
-        w_rest = held.tile([P, features - P], BF16, name="w_rest")
+        w_rest = held.tile([P, features - P], BF16, name="w_rest", align_bytes=DMA_ALIGN)
         nc.sync.dma_start(w_rest[:], w[:, P:features])
         w_blocks = [w_first[:]] + [w_rest[:, (a - 1) * P : a * P] for a in range(1, blocks)]
 
@@ -57,7 +59,7 @@ def tile_scatter_matmul_kernel(tc, base, x, w, offs, out):
             )
 
         for a in range(blocks):
-            z_tile = held.tile([P, tokens], F32, name=f"z{a}")
+            z_tile = held.tile([P, tokens], F32, name=f"z{a}", align_bytes=DMA_ALIGN)
             if a % 2 == 0:
                 nc.vector.tensor_copy(z_tile[:], windows[a][:])
                 nc.sync.dma_start(out[a * P : (a + 1) * P, :], z_tile[:])

@@ -39,11 +39,9 @@ def tile_scatter_matmul_kernel(tc, base, x, w, offs, out):
             nc.sync.dma_start(base_tiles[a][:], base[a * P : (a + 1) * P, :])
         x_tile = held.tile([P, entries], BF16, name="x_tile", align_bytes=DMA_ALIGN)
         nc.sync.dma_start(x_tile[:], x)
-        w_first = held.tile([P, P], BF16, name="w_first", align_bytes=DMA_ALIGN)
-        nc.sync.dma_start(w_first[:], w[:, 0:P])
-        w_rest = held.tile([P, features - P], BF16, name="w_rest", align_bytes=DMA_ALIGN)
-        nc.sync.dma_start(w_rest[:], w[:, P:features])
-        w_blocks = [w_first[:]] + [w_rest[:, (a - 1) * P : a * P] for a in range(1, blocks)]
+        w_tiles = [held.tile([P, P], BF16, name=f"w{a}", align_bytes=DMA_ALIGN) for a in range(blocks)]
+        for a in range(blocks):
+            nc.sync.dma_start(w_tiles[a][:], w[:, a * P : (a + 1) * P])
 
         windows = [banks.tile([P, tokens], F32, name=f"window{a}") for a in range(blocks)]
         for a in range(blocks):
@@ -52,7 +50,7 @@ def tile_scatter_matmul_kernel(tc, base, x, w, offs, out):
         for a in range(blocks):
             nc.tensor.matmul(
                 windows[a][:].indirect(offsets[:]),
-                w_blocks[a],
+                w_tiles[a][:],
                 x_tile[:],
                 start=True,
                 stop=True,

@@ -60,7 +60,6 @@ def tile_scatter_matmul_kernel(tc, base, x, w, offs, out):
             z_tile = held.tile([P, tokens], F32, name=f"z{a}", align_bytes=DMA_ALIGN)
             if a % 2 == 0:
                 nc.vector.tensor_copy(z_tile[:], windows[a][:])
-                nc.sync.dma_start(out[a * P : (a + 1) * P, :], z_tile[:])
             else:
                 nc.scalar.copy(z_tile[:], windows[a][:])
-                nc.scalar.dma_start(out[a * P : (a + 1) * P, :], z_tile[:])
+            nc.sync.dma_start(out[a * P : (a + 1) * P, :], z_tile[:])

import concourse.mybir as mybir
from concourse.masks import make_identity

P = 128
BF16, F32, U16 = mybir.dt.bfloat16, mybir.dt.float32, mybir.dt.uint16

FLOPS = 2 * 128 * 512 * 128

DMA_ALIGN = 256

WARM_COLUMNS = 128
WARM_MATMULS = 10


def tile_scatter_matmul_kernel(tc, base, x, w, offs, out):
    nc = tc.nc
    features, tokens = base.shape
    entries = x.shape[1]
    blocks = features // P

    with (
        tc.tile_pool(name="held", bufs=1) as held,
        tc.psum_pool(name="banks", bufs=1) as banks,
    ):
        offsets = held.tile([P, entries // 16], U16, name="offsets")
        nc.sync.dma_start(offsets[:], offs)

        zeros = held.tile([P, WARM_COLUMNS], BF16, name="zeros")
        nc.vector.memset(zeros[:], 0.0)
        spare = banks.tile([P, WARM_COLUMNS], F32, name="spare")
        for repeat in range(WARM_MATMULS):
            nc.tensor.matmul(spare[:], zeros[:, 0:P], zeros[:], start=True, stop=True)

        ident = held.tile([P, P], BF16, name="ident")
        make_identity(nc, ident[:])

        base_tiles = [held.tile([P, tokens], BF16, name=f"base{a}", align_bytes=DMA_ALIGN) for a in range(blocks)]
        for a in range(blocks):
            nc.sync.dma_start(base_tiles[a][:], base[a * P : (a + 1) * P, :])
        x_tile = held.tile([P, entries], BF16, name="x_tile", align_bytes=DMA_ALIGN)
        nc.sync.dma_start(x_tile[:], x)
        w_tiles = [held.tile([P, P], BF16, name=f"w{a}", align_bytes=DMA_ALIGN) for a in range(blocks)]
        for a in range(blocks):
            nc.sync.dma_start(w_tiles[a][:], w[:, a * P : (a + 1) * P])

        windows = [banks.tile([P, tokens], F32, name=f"window{a}") for a in range(blocks)]
        for a in range(blocks):
            nc.tensor.matmul(windows[a][:], ident[:], base_tiles[a][:], start=True, stop=True)

        for a in range(blocks):
            nc.tensor.matmul(
                windows[a][:].indirect(offsets[:]),
                w_tiles[a][:],
                x_tile[:],
                start=True,
                stop=True,
            )

        for a in range(blocks):
            z_tile = held.tile([P, tokens], F32, name=f"z{a}", align_bytes=DMA_ALIGN)
            if a % 2 == 0:
                nc.vector.tensor_copy(z_tile[:], windows[a][:])
            else:
                nc.scalar.copy(z_tile[:], windows[a][:])
            nc.sync.dma_start(out[a * P : (a + 1) * P, :], z_tile[:])
